import numpy as np
import ml_dtypes


def mxq(x, axis, fmt="e4m3"):
    dtype, down = {"e4m3": (ml_dtypes.float8_e4m3fn, 7), "e5m2": (ml_dtypes.float8_e5m2, 14)}[fmt]
    v = np.moveaxis(np.asarray(x, np.float32).astype(ml_dtypes.bfloat16).astype(np.float64), axis, -1)
    blocks = v.reshape(v.shape[:-1] + (-1, 32))
    amax = np.abs(blocks).max(-1, keepdims=True)
    byte = np.maximum(np.where(amax > 0, np.frexp(amax)[1] - 1 + 127, 0) - down, 1)
    scale = np.exp2(byte - 127.0)
    codes = (blocks / scale).astype(np.float32).astype(dtype).astype(np.float64)
    return np.moveaxis((codes * scale).reshape(v.shape), -1, axis)


WIDE = False


def mx_kscale(k):
    if not WIDE:
        return np.ones(k)
    levels = np.array([30, -30])
    if k % 512:
        return np.exp2(np.random.permutation(np.resize(levels, k // 32))).repeat(32)
    a = np.empty((k // 512, 16))
    for p in range(k // 512):
        a[p, :8] = np.random.permutation(np.resize(levels, 8))
        for g in range(8):
            far = levels[np.abs(levels - a[p, g]) >= 10]
            a[p, g + 8] = far[np.random.randint(len(far))]
    return np.exp2(a.ravel()).repeat(32)


def f64(x):
    return np.asarray(x).astype(np.float64)


def striped(idx):
    return np.tile(np.asarray(idx).reshape(-1, 16).T, (8, 1)).astype(np.uint16)


def unstriped(offs):
    return offs[:16].T.reshape(-1).astype(np.int64)


E2M1 = np.array([0.0, 0.5, 1.0, 1.5, 2.0, 3.0, 4.0, 6.0, -0.0, -0.5, -1.0, -1.5, -2.0, -3.0, -4.0, -6.0])


def pack_weight(w, fmt):
    k, n = w.shape
    w = f64(np.asarray(w, np.float32).astype(ml_dtypes.bfloat16)).reshape(k // 32, 32, n)
    amax = np.abs(w).max(1)
    if fmt in ("e4m3", "e5m2"):
        byte = np.frexp(amax)[1] - 1 + 127 - (7 if fmt == "e4m3" else 14)
    else:
        mant, ex = np.frexp(amax / 6.0)
        byte = np.where(mant > 0.5, ex, ex - 1) + 127
    byte = np.clip(np.where(amax > 0, byte, 1), 1, 254)
    scaled = (w * np.exp2(127.0 - byte)[:, None, :]).reshape(k, n).astype(np.float32)
    by_word = np.ascontiguousarray(scaled.reshape(k // 512, 128, 4, n).transpose(0, 1, 3, 2))
    if fmt in ("e4m3", "e5m2"):
        words = by_word.astype(ml_dtypes.float8_e4m3fn if fmt == "e4m3" else ml_dtypes.float8_e5m2).view(np.uint8)
    else:
        c = by_word.astype(ml_dtypes.float4_e2m1fn).view(np.uint8) & 0xF
        words = (c[..., 0::2] | (c[..., 1::2] << 4)).reshape(k // 512, 128, 2 * n)
    return np.ascontiguousarray(words), np.ascontiguousarray(byte.astype(np.uint8).reshape(k // 512, 16, n))


def unpack_weight(words, scales, fmt):
    g, _, n = scales.shape
    words = np.ascontiguousarray(words).reshape(g, 128, n, -1)
    if fmt in ("e4m3", "e5m2"):
        vals = words.view(ml_dtypes.float8_e4m3fn if fmt == "e4m3" else ml_dtypes.float8_e5m2).astype(np.float64)
    else:
        nib = np.empty((g, 128, n, 4), np.uint8)
        nib[..., 0::2] = words & 0xF
        nib[..., 1::2] = words >> 4
        vals = E2M1[nib]
    vals = vals * np.repeat(np.exp2(scales.astype(np.float64) - 127.0), 8, axis=1)[..., None]
    return vals.transpose(0, 1, 3, 2).reshape(g * 512, n)


K, T, J, S, R, V, N = 1024, 1024, 384, 512, 512, 512, 256


def setup_inputs():
    n = np.random.standard_normal
    idx = np.random.permutation(T)[:J]
    idx2 = np.random.permutation(S)[:J]
    idx3 = np.random.permutation(V)[:J]
    idx4 = np.random.permutation(V)[:J]
    fk = mx_kscale(K)
    fr = mx_kscale(R)
    wp = pack_weight(n((K, R)) * 1 / np.sqrt(K) * fk[:, None] * fr, "e5m2")
    wbp = pack_weight(n((R, N)) * 1 / np.sqrt(R) / fr[:, None], "e5m2")
    return {
        "xa": (n((K, T))).astype(np.float32),
        "xb": (n((K, S))).astype(np.float32),
        "hb": (np.random.uniform(0.2, 0.9, (K, 1))).astype(np.float32),
        "fk": (np.random.uniform(0.5, 2.0, (K, 1)) / fk[:, None]).astype(np.float32),
        "w_words": wp[0],
        "w_scales": wp[1],
        "tb": (n((R, V)) * 0.7 * fr[:, None]).astype(np.float32),
        "wb_words": wbp[0],
        "wb_scales": wbp[1],
        "bi": (np.random.uniform(-0.5, 0.5, (1, N))).astype(np.float32),
        "offs": striped(idx),
        "offs2": striped(idx2),
        "offs3": striped(idx3),
        "offs4": striped(idx4),
    }


def reference(xa, xb, hb, fk, w_words, w_scales, tb, wb_words, wb_scales, bi, offs, offs2, offs3, offs4):
    idx = unstriped(offs)
    idx2 = unstriped(offs2)
    idx3 = unstriped(offs3)
    idx4 = unstriped(offs4)
    wu = unpack_weight(w_words, w_scales, "e5m2")
    wbu = unpack_weight(wb_words, wb_scales, "e5m2")
    u = (f64(xa)[:, idx] - np.minimum(f64(xb)[:, idx2], f64(hb))) * f64(fk)
    uq = mxq(u, 0, "e4m3")
    a = wu.T @ uq
    hid = np.maximum(a + f64(tb)[:, idx3] - f64(tb)[:, idx4], 0.0)
    hidq = mxq(hid, 0, "e4m3")
    p = hidq.T @ wbu
    ea = np.exp(0.7 * p + f64(bi))
    y = 256.0 * ea / np.sum(ea, axis=1, keepdims=True)
    return y

@@ -1,0 +1,212 @@
+from contextlib import ExitStack
+
+import concourse.mybir as mybir
+from concourse.masks import make_identity
+
+K, T, J, S, R, V, N = 1024, 1024, 384, 512, 512, 512, 256
+FLOPS = 2 * K * R * J + 2 * J * R * N
+
+F32 = mybir.dt.float32
+BF16 = mybir.dt.bfloat16
+U32 = mybir.dt.uint32
+I32 = mybir.dt.int32
+U16 = mybir.dt.uint16
+U8 = mybir.dt.uint8
+E4 = mybir.dt.float8_e4m3fn_x4
+E5 = mybir.dt.float8_e5m2_x4
+ALU = mybir.AluOpType
+ACT = mybir.ActivationFunctionType
+
+P = 128
+PACK = 4
+PASSES = K // (P * PACK)
+CHUNK = 128
+CHUNKS = J // CHUNK
+HALF = J // 2
+VECTOR_XA = (1, 3, 5)
+
+
+def tile_list_boundedgaps_tworeach_rowshares_kernel(
+    tc, xa, xb, hb, fk, w_words, w_scales, tb, wb_words, wb_scales, bi, offs, offs2, offs3, offs4, out
+):
+    nc = tc.nc
+    with ExitStack() as ctx:
+        keep = ctx.enter_context(tc.tile_pool(name="keep", bufs=1))
+        psum = ctx.enter_context(tc.psum_pool(name="psum", bufs=1))
+
+        def tile(shape, dtype, name):
+            return keep.tile(shape, dtype, name=name, align_bytes=64)
+
+        lists = {}
+        for name in ("offs", "offs2", "offs3", "offs4"):
+            lists[name] = tile([P, J // 16], U16, name)
+
+        xa_rows = xa.rearrange("(z p t) c -> z t p c", z=PASSES, t=PACK)
+        xb_rows = xb.rearrange("(z p t) c -> z t p c", z=PASSES, t=PACK)
+        tb_rows = tb.rearrange("(p t) c -> t p c", t=PACK)
+        planes = PASSES * PACK
+        xa_sb = [tile([P, T], F32, "xa%d" % g) for g in range(planes)]
+        xb_sb = [tile([P, S], F32, "xb%d" % g) for g in range(planes)]
+        tb_sb = [tile([P, V], F32, "tb%d" % t) for t in range(PACK)]
+        w_raw = [tile([P, R], U32, "w_raw%d" % z) for z in range(PASSES)]
+        w_codes = [tile([P, R], U32, "w_codes%d" % z) for z in range(PASSES)]
+        ws_raw = tile([P, PASSES * R], U8, "ws_raw")
+        ws = tile([P, PASSES * R], U8, "ws")
+        wb_codes = tile([P, N], U32, "wb_codes")
+        wbs = tile([P, N], U8, "wbs")
+        hb_sb = tile([P, planes], F32, "hb_sb")
+        fk_sb = tile([P, planes], F32, "fk_sb")
+        neg_fk = tile([P, planes], F32, "neg_fk")
+        bi_col = tile([P, 2], F32, "bi_col")
+        bi_all = tile([P, N], F32, "bi_all")
+        ident = tile([P, P], F32, "ident")
+
+        nc.vector.memset(ws_raw[:].bitcast(I32), 0)
+        nc.vector.memset(wbs[:].bitcast(I32), 0)
+
+        def load_words(dst, words):
+            nc.sync.dma_start(dst[:].bitcast(I32), words.rearrange("p n t -> p (n t)").bitcast(I32))
+
+        def load_per_k(dst, src):
+            nc.sync.dma_start(
+                dst[:].rearrange("p (z t) -> p z t", t=PACK), src.rearrange("(z p t) o -> p z (t o)", z=PASSES, t=PACK)
+            )
+
+        nc.sync.dma_start(lists["offs4"][:], offs4)
+        nc.sync.dma_start(tb_sb[0][:], tb_rows[0])
+        nc.sync.dma_start(lists["offs3"][:], offs3)
+        for t in range(1, PACK):
+            nc.sync.dma_start(tb_sb[t][:], tb_rows[t])
+        nc.sync.dma_start(lists["offs2"][:], offs2)
+        for g in range(planes):
+            z, t = divmod(g, PACK)
+            if g == planes - 1:
+                nc.sync.dma_start(xa_sb[g][:], xa_rows[z, t])
+                nc.sync.dma_start(xb_sb[g][:], xb_rows[z, t])
+            else:
+                nc.sync.dma_start(xb_sb[g][:], xb_rows[z, t])
+                if g == 0:
+                    nc.sync.dma_start(lists["offs"][:], offs)
+                nc.sync.dma_start(xa_sb[g][:], xa_rows[z, t])
+            if g == 0:
+                load_per_k(hb_sb, hb)
+            if g == 1:
+                load_per_k(fk_sb, fk)
+                nc.sync.dma_start(bi_col[:], bi.rearrange("o (p h) -> p (o h)", h=2))
+            if g == 2:
+                for q in range(4):
+                    nc.sync.dma_start(
+                        ws_raw[32 * q : 32 * q + 4, :].bitcast(I32).rearrange("r (z c) -> r z c", z=PASSES),
+                        w_scales[:, 4 * q : 4 * q + 4, :].bitcast(I32).rearrange("z r c -> r z c"),
+                    )
+            if t == PACK - 1:
+                load_words(w_raw[z], w_words[z])
+        load_words(wb_codes, wb_words[0])
+        for q in range(4):
+            nc.sync.dma_start(
+                wbs[32 * q : 32 * q + 4, :].bitcast(I32), wb_scales[0, 4 * q : 4 * q + 4, :].bitcast(I32)
+            )
+
+        make_identity(nc, ident[:])
+
+        tb_off = tile([P, PACK, J], F32, "tb_off")
+        tb_diff = tile([P, PACK, J], F32, "tb_diff")
+        for t in range(PACK):
+            nc.scalar.activation(tb_off[:, t, :], tb_sb[t][:].indirect(lists["offs4"][:]), ACT.Copy)
+            for h in range(2):
+                nc.vector.tensor_tensor(
+                    tb_diff[:, t, h * HALF : (h + 1) * HALF],
+                    tb_sb[t][:].indirect(lists["offs3"][:, h * HALF // 16 : (h + 1) * HALF // 16]),
+                    tb_off[:, t, h * HALF : (h + 1) * HALF],
+                    ALU.subtract,
+                )
+
+        nc.vector.tensor_scalar(neg_fk[:], fk_sb[:], -1.0, None, ALU.mult)
+        bi_ps = psum.tile([P, 2, P], F32, name="bi_ps")
+        for h in range(2):
+            nc.tensor.transpose(bi_ps[:, h, :], bi_col[:, h : h + 1].to_broadcast([P, P]), ident[:])
+        nc.vector.tensor_copy(bi_all[:].rearrange("q (p h) -> q p h", h=2), bi_ps[:].rearrange("q h p -> q p h"))
+        nc.vector.tensor_copy(
+            ws[:].rearrange("p (z t m) -> p z t m", z=PASSES, t=PACK),
+            ws_raw[:].rearrange("p (z m t) -> p z t m", z=PASSES, t=PACK),
+        )
+
+        def weave(dst, planes_in, other):
+            return (
+                dst.rearrange("p (c i t) -> p c t i", i=2, t=PACK),
+                planes_in.rearrange("p t (c i) -> p c t i", i=2),
+                other,
+            )
+
+        a_ps = [psum.tile([P, PACK, CHUNK], F32, name="a_ps%d" % c) for c in range(CHUNKS)]
+        for z in range(PASSES):
+            gap = tile([P, PACK, J], F32, "gap%d" % z)
+            for t in range(PACK):
+                g = z * PACK + t
+                xa_got = tile([P, J], F32, "xa_got%d" % g)
+                xb_got = tile([P, J], F32, "xb_got%d" % g)
+                nc.scalar.activation(xb_got[:], xb_sb[g][:].indirect(lists["offs2"][:]), ACT.Copy)
+                if g in VECTOR_XA:
+                    nc.vector.tensor_copy(xa_got[:], xa_sb[g][:].indirect(lists["offs"][:]))
+                else:
+                    nc.scalar.activation(xa_got[:], xa_sb[g][:].indirect(lists["offs"][:]), ACT.Copy)
+                nc.vector.scalar_tensor_tensor(
+                    gap[:, t, :], xb_got[:], hb_sb[:, g : g + 1], xa_got[:], ALU.min, ALU.subtract
+                )
+            nc.scalar.copy(
+                w_codes[z][:].rearrange("p (t m) -> p t m", t=PACK), w_raw[z][:].rearrange("p (m t) -> p t m", t=PACK)
+            )
+            width = J if z < PASSES - 1 else CHUNK
+            for j0 in range(0, J, width):
+                u_bf = tile([P, PACK * width], BF16, "u_bf%d_%d" % (z, j0))
+                u_codes = tile([P, width], U32, "u_codes%d_%d" % (z, j0))
+                u_sc = tile([P, width], U8, "u_sc%d_%d" % (z, j0))
+                factor = neg_fk[:, z * PACK : (z + 1) * PACK].unsqueeze(1).unsqueeze(3).to_broadcast([P, width // 2, PACK, 2])
+                o, i0, i1 = weave(u_bf[:], gap[:, :, j0 : j0 + width], factor)
+                nc.vector.tensor_tensor(o, i0, i1, ALU.mult)
+                nc.vector.quantize_mx(out=u_codes[:].bitcast(E4), scales=u_sc[:], in_=u_bf[:])
+                for c in range(j0 // CHUNK, (j0 + width) // CHUNK):
+                    cols = slice(c * CHUNK - j0, (c + 1) * CHUNK - j0)
+                    for t in range(PACK):
+                        nc.tensor.matmul_mx(
+                            out=a_ps[c][:, t, :],
+                            lhsT=w_codes[z][:, t * P : (t + 1) * P].bitcast(E5),
+                            lhsT_scale=ws[:, z * R + t * P : z * R + (t + 1) * P],
+                            rhs=u_codes[:, cols].bitcast(E4),
+                            rhs_scale=u_sc[:, cols],
+                            start=(z == 0 and t == 0),
+                            stop=(z == PASSES - 1 and t == PACK - 1),
+                        )
+
+        for c in range(CHUNKS):
+            cols = slice(c * CHUNK, (c + 1) * CHUNK)
+            pre = tile([P, PACK * CHUNK], BF16, "pre%d" % c)
+            hid = tile([P, PACK * CHUNK], BF16, "hid%d" % c)
+            h_codes = tile([P, CHUNK], U32, "h_codes%d" % c)
+            h_sc = tile([P, CHUNK], U8, "h_sc%d" % c)
+            o, i0, i1 = weave(pre[:], a_ps[c][:], tb_diff[:, :, cols].rearrange("p t (c i) -> p c t i", i=2))
+            nc.vector.tensor_tensor(o, i0, i1, ALU.add)
+            nc.vector.tensor_scalar(hid[:], pre[:], 0.0, None, ALU.max)
+            nc.vector.quantize_mx(out=h_codes[:].bitcast(E4), scales=h_sc[:], in_=hid[:])
+            p_ps = psum.tile([P, N], F32, name="p_ps%d" % c)
+            nc.tensor.matmul_mx(
+                out=p_ps[:],
+                lhsT=h_codes[:].bitcast(E4),
+                lhsT_scale=h_sc[:],
+                rhs=wb_codes[:].bitcast(E5),
+                rhs_scale=wbs[:],
+                start=True,
+                stop=True,
+            )
+            neg_z = tile([P, N], F32, "neg_z%d" % c)
+            low = tile([P, 1], F32, "low%d" % c)
+            ea = tile([P, N], F32, "ea%d" % c)
+            total = tile([P, 1], F32, "total%d" % c)
+            inv = tile([P, 1], F32, "inv%d" % c)
+            y = tile([P, N], F32, "y%d" % c)
+            nc.vector.scalar_tensor_tensor(neg_z[:], p_ps[:], -0.7, bi_all[:], ALU.mult, ALU.subtract)
+            nc.vector.tensor_reduce(low[:], neg_z[:], mybir.AxisListType.X, ALU.min)
+            nc.scalar.activation(ea[:], neg_z[:], ACT.Exp, bias=low[:], scale=-1.0, accum_out=total[:])
+            nc.vector.reciprocal(inv[:], total[:])
+            nc.vector.tensor_scalar(y[:], ea[:], inv[:], 256.0, ALU.mult, ALU.mult)
+            nc.sync.dma_start(out[cols, :], y[:])

@@ -1,7 +1,6 @@
 from contextlib import ExitStack
 
 import concourse.mybir as mybir
-from concourse.masks import make_identity
 
 K, T, J, S, R, V, N = 1024, 1024, 384, 512, 512, 512, 256
 FLOPS = 2 * K * R * J + 2 * J * R * N
@@ -20,9 +19,9 @@ ACT = mybir.ActivationFunctionType
 P = 128
 PACK = 4
 PASSES = K // (P * PACK)
+PLANES = PASSES * PACK
 CHUNK = 128
 CHUNKS = J // CHUNK
-HALF = J // 2
 VECTOR_XA = (1, 3, 5)
 
 
@@ -41,28 +40,41 @@ def tile_list_boundedgaps_tworeach_rowshares_kernel(
         for name in ("offs", "offs2", "offs3", "offs4"):
             lists[name] = tile([P, J // 16], U16, name)
 
-        xa_rows = xa.rearrange("(z p t) c -> z t p c", z=PASSES, t=PACK)
-        xb_rows = xb.rearrange("(z p t) c -> z t p c", z=PASSES, t=PACK)
-        tb_rows = tb.rearrange("(p t) c -> t p c", t=PACK)
-        planes = PASSES * PACK
-        xa_sb = [tile([P, T], F32, "xa%d" % g) for g in range(planes)]
-        xb_sb = [tile([P, S], F32, "xb%d" % g) for g in range(planes)]
+        xa_rows = xa.rearrange("(q p t) c -> q p (t c)", p=P, t=PACK)
+        xb_rows = xb.rearrange("(q p t) c -> q p (t c)", p=P, t=PACK)
+        tb_rows = tb.rearrange("(p t) c -> p (t c)", t=PACK)
+        xa_groups = [(0, 2), (2, 4), (4, 6), (6, 7), (7, 8)]
+        xa_sb = [tile([P, (g1 - g0) * T], F32, "xa%d" % g0) for g0, g1 in xa_groups]
+        xb_sb = [tile([P, PACK * S], F32, "xb%d" % z) for z in range(PASSES)]
         tb_sb = [tile([P, V], F32, "tb%d" % t) for t in range(PACK)]
+
+        def xa_window(g):
+            for (g0, g1), held in zip(xa_groups, xa_sb):
+                if g0 <= g < g1:
+                    return held[:, (g - g0) * T : (g - g0 + 1) * T]
+
+        def load_xa(i):
+            g0, g1 = xa_groups[i]
+            z, t = divmod(g0, PACK)
+            nc.sync.dma_start(xa_sb[i][:], xa_rows[z, :, t * T : (t + g1 - g0) * T])
+
         w_raw = [tile([P, R], U32, "w_raw%d" % z) for z in range(PASSES)]
         w_codes = [tile([P, R], U32, "w_codes%d" % z) for z in range(PASSES)]
         ws_raw = tile([P, PASSES * R], U8, "ws_raw")
         ws = tile([P, PASSES * R], U8, "ws")
         wb_codes = tile([P, N], U32, "wb_codes")
         wbs = tile([P, N], U8, "wbs")
-        hb_sb = tile([P, planes], F32, "hb_sb")
-        fk_sb = tile([P, planes], F32, "fk_sb")
-        neg_fk = tile([P, planes], F32, "neg_fk")
-        bi_col = tile([P, 2], F32, "bi_col")
+        hb_sb = tile([P, PLANES], F32, "hb_sb")
+        fk_sb = tile([P, PLANES], F32, "fk_sb")
+        neg_fk = tile([P, PLANES], F32, "neg_fk")
         bi_all = tile([P, N], F32, "bi_all")
-        ident = tile([P, P], F32, "ident")
 
-        nc.vector.memset(ws_raw[:].bitcast(I32), 0)
-        nc.vector.memset(wbs[:].bitcast(I32), 0)
+        nc.gpsimd.memset(ws_raw[:].bitcast(I32), 0)
+        nc.gpsimd.memset(wbs[:].bitcast(I32), 0)
+        warm_in = tile([P, 1], F32, "warm_in")
+        warm_out = tile([P, 1], F32, "warm_out")
+        nc.gpsimd.memset(warm_in[:], 0.0)
+        nc.scalar.activation(warm_out[:], warm_in[:], ACT.Exp)
 
         def load_words(dst, words):
             nc.sync.dma_start(dst[:].bitcast(I32), words.rearrange("p n t -> p (n t)").bitcast(I32))
@@ -73,120 +85,142 @@ def tile_list_boundedgaps_tworeach_rowshares_kernel(
             )
 
         nc.sync.dma_start(lists["offs4"][:], offs4)
-        nc.sync.dma_start(tb_sb[0][:], tb_rows[0])
+        nc.sync.dma_start(tb_sb[0][:], tb_rows[:, 0:V])
         nc.sync.dma_start(lists["offs3"][:], offs3)
         for t in range(1, PACK):
-            nc.sync.dma_start(tb_sb[t][:], tb_rows[t])
+            nc.sync.dma_start(tb_sb[t][:], tb_rows[:, t * V : (t + 1) * V])
         nc.sync.dma_start(lists["offs2"][:], offs2)
-        for g in range(planes):
-            z, t = divmod(g, PACK)
-            if g == planes - 1:
-                nc.sync.dma_start(xa_sb[g][:], xa_rows[z, t])
-                nc.sync.dma_start(xb_sb[g][:], xb_rows[z, t])
-            else:
-                nc.sync.dma_start(xb_sb[g][:], xb_rows[z, t])
-                if g == 0:
-                    nc.sync.dma_start(lists["offs"][:], offs)
-                nc.sync.dma_start(xa_sb[g][:], xa_rows[z, t])
-            if g == 0:
-                load_per_k(hb_sb, hb)
-            if g == 1:
-                load_per_k(fk_sb, fk)
-                nc.sync.dma_start(bi_col[:], bi.rearrange("o (p h) -> p (o h)", h=2))
-            if g == 2:
-                for q in range(4):
-                    nc.sync.dma_start(
-                        ws_raw[32 * q : 32 * q + 4, :].bitcast(I32).rearrange("r (z c) -> r z c", z=PASSES),
-                        w_scales[:, 4 * q : 4 * q + 4, :].bitcast(I32).rearrange("z r c -> r z c"),
-                    )
-            if t == PACK - 1:
-                load_words(w_raw[z], w_words[z])
+        nc.sync.dma_start(xb_sb[0][:], xb_rows[0])
+        nc.sync.dma_start(lists["offs"][:], offs)
+        load_xa(0)
+        load_per_k(hb_sb, hb)
+        load_per_k(fk_sb, fk)
+        load_xa(1)
+        for q in range(4):
+            nc.sync.dma_start(
+                ws_raw[32 * q : 32 * q + 4, :].bitcast(I32).rearrange("r (z c) -> r z c", z=PASSES),
+                w_scales[:, 4 * q : 4 * q + 4, :].bitcast(I32).rearrange("z r c -> r z c"),
+            )
+        nc.sync.dma_start(xb_sb[1][:], xb_rows[1])
+        load_words(w_raw[0], w_words[0])
+        for i in range(2, len(xa_groups)):
+            load_xa(i)
+        load_words(w_raw[1], w_words[1])
         load_words(wb_codes, wb_words[0])
         for q in range(4):
             nc.sync.dma_start(
                 wbs[32 * q : 32 * q + 4, :].bitcast(I32), wb_scales[0, 4 * q : 4 * q + 4, :].bitcast(I32)
             )
+        nc.sync.dma_start(bi_all[:], bi[0].partition_broadcast(P))
 
-        make_identity(nc, ident[:])
-
-        tb_off = tile([P, PACK, J], F32, "tb_off")
+        tb_neg = tile([P, PACK, J], F32, "tb_neg")
         tb_diff = tile([P, PACK, J], F32, "tb_diff")
         for t in range(PACK):
-            nc.scalar.activation(tb_off[:, t, :], tb_sb[t][:].indirect(lists["offs4"][:]), ACT.Copy)
-            for h in range(2):
+            nc.scalar.activation(tb_neg[:, t, :], tb_sb[t][:].indirect(lists["offs4"][:]), ACT.Copy, scale=-1.0)
+            if t == 0:
+                tb_pos = tile([P, J], F32, "tb_pos")
+                nc.vector.tensor_copy(tb_pos[:], tb_sb[t][:].indirect(lists["offs3"][:]))
+                nc.vector.tensor_tensor(tb_diff[:, t, :], tb_pos[:], tb_neg[:, t, :], ALU.add)
+            else:
                 nc.vector.tensor_tensor(
-                    tb_diff[:, t, h * HALF : (h + 1) * HALF],
-                    tb_sb[t][:].indirect(lists["offs3"][:, h * HALF // 16 : (h + 1) * HALF // 16]),
-                    tb_off[:, t, h * HALF : (h + 1) * HALF],
-                    ALU.subtract,
+                    tb_diff[:, t, :], tb_sb[t][:].indirect(lists["offs3"][:]), tb_neg[:, t, :], ALU.add
                 )
 
-        nc.vector.tensor_scalar(neg_fk[:], fk_sb[:], -1.0, None, ALU.mult)
-        bi_ps = psum.tile([P, 2, P], F32, name="bi_ps")
-        for h in range(2):
-            nc.tensor.transpose(bi_ps[:, h, :], bi_col[:, h : h + 1].to_broadcast([P, P]), ident[:])
-        nc.vector.tensor_copy(bi_all[:].rearrange("q (p h) -> q p h", h=2), bi_ps[:].rearrange("q h p -> q p h"))
+        nc.gpsimd.tensor_scalar(neg_fk[:], fk_sb[:], -1.0, 0.0, ALU.mult, ALU.add)
         nc.vector.tensor_copy(
             ws[:].rearrange("p (z t m) -> p z t m", z=PASSES, t=PACK),
             ws_raw[:].rearrange("p (z m t) -> p z t m", z=PASSES, t=PACK),
         )
 
-        def weave(dst, planes_in, other):
-            return (
-                dst.rearrange("p (c i t) -> p c t i", i=2, t=PACK),
-                planes_in.rearrange("p t (c i) -> p c t i", i=2),
-                other,
+        def permute_w(z):
+            nc.scalar.copy(
+                w_codes[z][:].rearrange("p (t m) -> p t m", t=PACK), w_raw[z][:].rearrange("p (m t) -> p t m", t=PACK)
             )
 
+        def woven(dst, run):
+            return dst.rearrange("p (c i t) -> p c t i", i=run, t=PACK)
+
+        def by_plane(src, run):
+            return src.rearrange("p t (c i) -> p c t i", i=run)
+
+        def list_slice(name, cols):
+            return lists[name][:, cols.start // 16 : cols.stop // 16]
+
+        def product(z, u_bf, j0, width):
+            u_codes = tile([P, width], U32, "u_codes%d_%d" % (z, j0))
+            u_sc = tile([P, width], U8, "u_sc%d_%d" % (z, j0))
+            nc.vector.quantize_mx(out=u_codes[:].bitcast(E4), scales=u_sc[:], in_=u_bf[:])
+            for c in range(j0 // CHUNK, (j0 + width) // CHUNK):
+                cols = slice(c * CHUNK - j0, (c + 1) * CHUNK - j0)
+                for t in range(PACK):
+                    nc.tensor.matmul_mx(
+                        out=a_ps[c][:, t, :],
+                        lhsT=w_codes[z][:, t * P : (t + 1) * P].bitcast(E5),
+                        lhsT_scale=ws[:, z * R + t * P : z * R + (t + 1) * P],
+                        rhs=u_codes[:, cols].bitcast(E4),
+                        rhs_scale=u_sc[:, cols],
+                        start=(z == 0 and t == 0),
+                        stop=(z == PASSES - 1 and t == PACK - 1),
+                    )
+
         a_ps = [psum.tile([P, PACK, CHUNK], F32, name="a_ps%d" % c) for c in range(CHUNKS)]
+        chunk_cols = [slice(c * CHUNK, (c + 1) * CHUNK) for c in range(CHUNKS)]
         for z in range(PASSES):
             gap = tile([P, PACK, J], F32, "gap%d" % z)
+            u_planes = tile([P, PACK, J], BF16, "u_planes") if z == PASSES - 1 else None
             for t in range(PACK):
                 g = z * PACK + t
                 xa_got = tile([P, J], F32, "xa_got%d" % g)
                 xb_got = tile([P, J], F32, "xb_got%d" % g)
-                nc.scalar.activation(xb_got[:], xb_sb[g][:].indirect(lists["offs2"][:]), ACT.Copy)
-                if g in VECTOR_XA:
-                    nc.vector.tensor_copy(xa_got[:], xa_sb[g][:].indirect(lists["offs"][:]))
+                if t == PACK - 1:
+                    nc.vector.tensor_copy(xb_got[:], xb_sb[z][:, t * S :].indirect(lists["offs2"][:]))
                 else:
-                    nc.scalar.activation(xa_got[:], xa_sb[g][:].indirect(lists["offs"][:]), ACT.Copy)
-                nc.vector.scalar_tensor_tensor(
-                    gap[:, t, :], xb_got[:], hb_sb[:, g : g + 1], xa_got[:], ALU.min, ALU.subtract
+                    nc.scalar.activation(
+                        xb_got[:], xb_sb[z][:, t * S : (t + 2) * S].indirect(lists["offs2"][:]), ACT.Copy
+                    )
+                pieces = chunk_cols if g == PLANES - 1 else [slice(0, J)]
+                for cols in pieces:
+                    if g in VECTOR_XA:
+                        nc.vector.tensor_copy(xa_got[:, cols], xa_window(g).indirect(list_slice("offs", cols)))
+                    else:
+                        nc.scalar.activation(xa_got[:, cols], xa_window(g).indirect(list_slice("offs", cols)), ACT.Copy)
+                    nc.vector.scalar_tensor_tensor(
+                        gap[:, t, cols], xb_got[:, cols], hb_sb[:, g : g + 1], xa_got[:, cols], ALU.min, ALU.subtract
+                    )
+                    if z == PASSES - 1:
+                        nc.vector.tensor_scalar(u_planes[:, t, cols], gap[:, t, cols], neg_fk[:, g : g + 1], None, ALU.mult)
+            permute_w(z)
+            if z < PASSES - 1:
+                u_bf = tile([P, PACK * J], BF16, "u_bf")
+                factor = neg_fk[:, z * PACK : (z + 1) * PACK].unsqueeze(1).unsqueeze(3)
+                nc.vector.tensor_tensor(
+                    woven(u_bf[:], 2), by_plane(gap[:], 2), factor.to_broadcast([P, J // 2, PACK, 2]), ALU.mult
                 )
-            nc.scalar.copy(
-                w_codes[z][:].rearrange("p (t m) -> p t m", t=PACK), w_raw[z][:].rearrange("p (m t) -> p t m", t=PACK)
-            )
-            width = J if z < PASSES - 1 else CHUNK
-            for j0 in range(0, J, width):
-                u_bf = tile([P, PACK * width], BF16, "u_bf%d_%d" % (z, j0))
-                u_codes = tile([P, width], U32, "u_codes%d_%d" % (z, j0))
-                u_sc = tile([P, width], U8, "u_sc%d_%d" % (z, j0))
-                factor = neg_fk[:, z * PACK : (z + 1) * PACK].unsqueeze(1).unsqueeze(3).to_broadcast([P, width // 2, PACK, 2])
-                o, i0, i1 = weave(u_bf[:], gap[:, :, j0 : j0 + width], factor)
-                nc.vector.tensor_tensor(o, i0, i1, ALU.mult)
-                nc.vector.quantize_mx(out=u_codes[:].bitcast(E4), scales=u_sc[:], in_=u_bf[:])
-                for c in range(j0 // CHUNK, (j0 + width) // CHUNK):
-                    cols = slice(c * CHUNK - j0, (c + 1) * CHUNK - j0)
-                    for t in range(PACK):
-                        nc.tensor.matmul_mx(
-                            out=a_ps[c][:, t, :],
-                            lhsT=w_codes[z][:, t * P : (t + 1) * P].bitcast(E5),
-                            lhsT_scale=ws[:, z * R + t * P : z * R + (t + 1) * P],
-                            rhs=u_codes[:, cols].bitcast(E4),
-                            rhs_scale=u_sc[:, cols],
-                            start=(z == 0 and t == 0),
-                            stop=(z == PASSES - 1 and t == PACK - 1),
-                        )
+                product(z, u_bf, 0, J)
+            else:
+                for c, cols in enumerate(chunk_cols):
+                    u_bf = tile([P, PACK * CHUNK], BF16, "u_last%d" % c)
+                    if c < 2:
+                        nc.vector.tensor_copy(woven(u_bf[:], 4), by_plane(u_planes[:, :, cols], 4))
+                    else:
+                        nc.scalar.copy(woven(u_bf[:], 4), by_plane(u_planes[:, :, cols], 4))
+                    product(z, u_bf, cols.start, CHUNK)
 
         for c in range(CHUNKS):
-            cols = slice(c * CHUNK, (c + 1) * CHUNK)
+            cols = chunk_cols[c]
             pre = tile([P, PACK * CHUNK], BF16, "pre%d" % c)
             hid = tile([P, PACK * CHUNK], BF16, "hid%d" % c)
             h_codes = tile([P, CHUNK], U32, "h_codes%d" % c)
             h_sc = tile([P, CHUNK], U8, "h_sc%d" % c)
-            o, i0, i1 = weave(pre[:], a_ps[c][:], tb_diff[:, :, cols].rearrange("p t (c i) -> p c t i", i=2))
-            nc.vector.tensor_tensor(o, i0, i1, ALU.add)
-            nc.vector.tensor_scalar(hid[:], pre[:], 0.0, None, ALU.max)
+            if c < 2:
+                pre_planes = pre[:].rearrange("p (t j) -> p t j", t=PACK)
+                nc.vector.tensor_tensor(pre_planes, a_ps[c][:], tb_diff[:, :, cols], ALU.add)
+                nc.scalar.activation(woven(hid[:], 4), by_plane(pre_planes, 4), ACT.Relu)
+            else:
+                nc.vector.tensor_tensor(
+                    woven(pre[:], 2), by_plane(a_ps[c][:], 2), by_plane(tb_diff[:, :, cols], 2), ALU.add
+                )
+                nc.vector.tensor_scalar(hid[:], pre[:], 0.0, None, ALU.max)
             nc.vector.quantize_mx(out=h_codes[:].bitcast(E4), scales=h_sc[:], in_=hid[:])
             p_ps = psum.tile([P, N], F32, name="p_ps%d" % c)
             nc.tensor.matmul_mx(

from contextlib import ExitStack

import concourse.mybir as mybir

K, T, J, S, R, V, N = 1024, 1024, 384, 512, 512, 512, 256
FLOPS = 2 * K * R * J + 2 * J * R * N

F32 = mybir.dt.float32
BF16 = mybir.dt.bfloat16
U32 = mybir.dt.uint32
I32 = mybir.dt.int32
U16 = mybir.dt.uint16
U8 = mybir.dt.uint8
E4 = mybir.dt.float8_e4m3fn_x4
E5 = mybir.dt.float8_e5m2_x4
ALU = mybir.AluOpType
ACT = mybir.ActivationFunctionType

P = 128
PACK = 4
PASSES = K // (P * PACK)
PLANES = PASSES * PACK
CHUNK = 128
CHUNKS = J // CHUNK
VECTOR_XA = (1, 3, 5)


def tile_list_boundedgaps_tworeach_rowshares_kernel(
    tc, xa, xb, hb, fk, w_words, w_scales, tb, wb_words, wb_scales, bi, offs, offs2, offs3, offs4, out
):
    nc = tc.nc
    with ExitStack() as ctx:
        keep = ctx.enter_context(tc.tile_pool(name="keep", bufs=1))
        psum = ctx.enter_context(tc.psum_pool(name="psum", bufs=1))

        def tile(shape, dtype, name):
            return keep.tile(shape, dtype, name=name, align_bytes=64)

        lists = {}
        for name in ("offs", "offs2", "offs3", "offs4"):
            lists[name] = tile([P, J // 16], U16, name)

        xa_rows = xa.rearrange("(q p t) c -> q p (t c)", p=P, t=PACK)
        xb_rows = xb.rearrange("(q p t) c -> q p (t c)", p=P, t=PACK)
        tb_rows = tb.rearrange("(p t) c -> p (t c)", t=PACK)
        xa_groups = [(0, 2), (2, 4), (4, 6), (6, 7), (7, 8)]
        xa_sb = [tile([P, (g1 - g0) * T], F32, "xa%d" % g0) for g0, g1 in xa_groups]
        xb_sb = [tile([P, PACK * S], F32, "xb%d" % z) for z in range(PASSES)]
        tb_sb = [tile([P, V], F32, "tb%d" % t) for t in range(PACK)]

        def xa_window(g):
            for (g0, g1), held in zip(xa_groups, xa_sb):
                if g0 <= g < g1:
                    return held[:, (g - g0) * T : (g - g0 + 1) * T]

        def load_xa(i):
            g0, g1 = xa_groups[i]
            z, t = divmod(g0, PACK)
            nc.sync.dma_start(xa_sb[i][:], xa_rows[z, :, t * T : (t + g1 - g0) * T])

        w_raw = [tile([P, R], U32, "w_raw%d" % z) for z in range(PASSES)]
        w_codes = [tile([P, R], U32, "w_codes%d" % z) for z in range(PASSES)]
        ws_raw = tile([P, PASSES * R], U8, "ws_raw")
        ws = tile([P, PASSES * R], U8, "ws")
        wb_codes = tile([P, N], U32, "wb_codes")
        wbs = tile([P, N], U8, "wbs")
        hb_sb = tile([P, PLANES], F32, "hb_sb")
        fk_sb = tile([P, PLANES], F32, "fk_sb")
        neg_fk = tile([P, PLANES], F32, "neg_fk")
        bi_all = tile([P, N], F32, "bi_all")

        nc.gpsimd.memset(ws_raw[:].bitcast(I32), 0)
        nc.gpsimd.memset(wbs[:].bitcast(I32), 0)
        warm_in = tile([P, 1], F32, "warm_in")
        warm_out = tile([P, 1], F32, "warm_out")
        nc.gpsimd.memset(warm_in[:], 0.0)
        nc.scalar.activation(warm_out[:], warm_in[:], ACT.Exp)

        def load_words(dst, words):
            nc.sync.dma_start(dst[:].bitcast(I32), words.rearrange("p n t -> p (n t)").bitcast(I32))

        def load_per_k(dst, src):
            nc.sync.dma_start(
                dst[:].rearrange("p (z t) -> p z t", t=PACK), src.rearrange("(z p t) o -> p z (t o)", z=PASSES, t=PACK)
            )

        nc.sync.dma_start(lists["offs4"][:], offs4)
        nc.sync.dma_start(tb_sb[0][:], tb_rows[:, 0:V])
        nc.sync.dma_start(lists["offs3"][:], offs3)
        for t in range(1, PACK):
            nc.sync.dma_start(tb_sb[t][:], tb_rows[:, t * V : (t + 1) * V])
        nc.sync.dma_start(lists["offs2"][:], offs2)
        nc.sync.dma_start(xb_sb[0][:], xb_rows[0])
        nc.sync.dma_start(lists["offs"][:], offs)
        load_xa(0)
        load_per_k(hb_sb, hb)
        load_per_k(fk_sb, fk)
        load_xa(1)
        for q in range(4):
            nc.sync.dma_start(
                ws_raw[32 * q : 32 * q + 4, :].bitcast(I32).rearrange("r (z c) -> r z c", z=PASSES),
                w_scales[:, 4 * q : 4 * q + 4, :].bitcast(I32).rearrange("z r c -> r z c"),
            )
        nc.sync.dma_start(xb_sb[1][:], xb_rows[1])
        load_words(w_raw[0], w_words[0])
        for i in range(2, len(xa_groups)):
            load_xa(i)
        load_words(w_raw[1], w_words[1])
        load_words(wb_codes, wb_words[0])
        for q in range(4):
            nc.sync.dma_start(
                wbs[32 * q : 32 * q + 4, :].bitcast(I32), wb_scales[0, 4 * q : 4 * q + 4, :].bitcast(I32)
            )
        nc.sync.dma_start(bi_all[:], bi[0].partition_broadcast(P))

        tb_neg = tile([P, PACK, J], F32, "tb_neg")
        tb_diff = tile([P, PACK, J], F32, "tb_diff")
        for t in range(PACK):
            nc.scalar.activation(tb_neg[:, t, :], tb_sb[t][:].indirect(lists["offs4"][:]), ACT.Copy, scale=-1.0)
            if t == 0:
                tb_pos = tile([P, J], F32, "tb_pos")
                nc.vector.tensor_copy(tb_pos[:], tb_sb[t][:].indirect(lists["offs3"][:]))
                nc.vector.tensor_tensor(tb_diff[:, t, :], tb_pos[:], tb_neg[:, t, :], ALU.add)
            else:
                nc.vector.tensor_tensor(
                    tb_diff[:, t, :], tb_sb[t][:].indirect(lists["offs3"][:]), tb_neg[:, t, :], ALU.add
                )

        nc.gpsimd.tensor_scalar(neg_fk[:], fk_sb[:], -1.0, 0.0, ALU.mult, ALU.add)
        nc.vector.tensor_copy(
            ws[:].rearrange("p (z t m) -> p z t m", z=PASSES, t=PACK),
            ws_raw[:].rearrange("p (z m t) -> p z t m", z=PASSES, t=PACK),
        )

        def permute_w(z):
            nc.scalar.copy(
                w_codes[z][:].rearrange("p (t m) -> p t m", t=PACK), w_raw[z][:].rearrange("p (m t) -> p t m", t=PACK)
            )

        def woven(dst, run):
            return dst.rearrange("p (c i t) -> p c t i", i=run, t=PACK)

        def by_plane(src, run):
            return src.rearrange("p t (c i) -> p c t i", i=run)

        def list_slice(name, cols):
            return lists[name][:, cols.start // 16 : cols.stop // 16]

        def product(z, u_bf, j0, width):
            u_codes = tile([P, width], U32, "u_codes%d_%d" % (z, j0))
            u_sc = tile([P, width], U8, "u_sc%d_%d" % (z, j0))
            nc.vector.quantize_mx(out=u_codes[:].bitcast(E4), scales=u_sc[:], in_=u_bf[:])
            for c in range(j0 // CHUNK, (j0 + width) // CHUNK):
                cols = slice(c * CHUNK - j0, (c + 1) * CHUNK - j0)
                for t in range(PACK):
                    nc.tensor.matmul_mx(
                        out=a_ps[c][:, t, :],
                        lhsT=w_codes[z][:, t * P : (t + 1) * P].bitcast(E5),
                        lhsT_scale=ws[:, z * R + t * P : z * R + (t + 1) * P],
                        rhs=u_codes[:, cols].bitcast(E4),
                        rhs_scale=u_sc[:, cols],
                        start=(z == 0 and t == 0),
                        stop=(z == PASSES - 1 and t == PACK - 1),
                    )

        a_ps = [psum.tile([P, PACK, CHUNK], F32, name="a_ps%d" % c) for c in range(CHUNKS)]
        chunk_cols = [slice(c * CHUNK, (c + 1) * CHUNK) for c in range(CHUNKS)]
        for z in range(PASSES):
            gap = tile([P, PACK, J], F32, "gap%d" % z)
            u_planes = tile([P, PACK, J], BF16, "u_planes") if z == PASSES - 1 else None
            for t in range(PACK):
                g = z * PACK + t
                xa_got = tile([P, J], F32, "xa_got%d" % g)
                xb_got = tile([P, J], F32, "xb_got%d" % g)
                if t == PACK - 1:
                    nc.vector.tensor_copy(xb_got[:], xb_sb[z][:, t * S :].indirect(lists["offs2"][:]))
                else:
                    nc.scalar.activation(
                        xb_got[:], xb_sb[z][:, t * S : (t + 2) * S].indirect(lists["offs2"][:]), ACT.Copy
                    )
                pieces = chunk_cols if g == PLANES - 1 else [slice(0, J)]
                for cols in pieces:
                    if g in VECTOR_XA:
                        nc.vector.tensor_copy(xa_got[:, cols], xa_window(g).indirect(list_slice("offs", cols)))
                    else:
                        nc.scalar.activation(xa_got[:, cols], xa_window(g).indirect(list_slice("offs", cols)), ACT.Copy)
                    nc.vector.scalar_tensor_tensor(
                        gap[:, t, cols], xb_got[:, cols], hb_sb[:, g : g + 1], xa_got[:, cols], ALU.min, ALU.subtract
                    )
                    if z == PASSES - 1:
                        nc.vector.tensor_scalar(u_planes[:, t, cols], gap[:, t, cols], neg_fk[:, g : g + 1], None, ALU.mult)
            permute_w(z)
            if z < PASSES - 1:
                u_bf = tile([P, PACK * J], BF16, "u_bf")
                factor = neg_fk[:, z * PACK : (z + 1) * PACK].unsqueeze(1).unsqueeze(3)
                nc.vector.tensor_tensor(
                    woven(u_bf[:], 2), by_plane(gap[:], 2), factor.to_broadcast([P, J // 2, PACK, 2]), ALU.mult
                )
                product(z, u_bf, 0, J)
            else:
                for c, cols in enumerate(chunk_cols):
                    u_bf = tile([P, PACK * CHUNK], BF16, "u_last%d" % c)
                    if c < 2:
                        nc.vector.tensor_copy(woven(u_bf[:], 4), by_plane(u_planes[:, :, cols], 4))
                    else:
                        nc.scalar.copy(woven(u_bf[:], 4), by_plane(u_planes[:, :, cols], 4))
                    product(z, u_bf, cols.start, CHUNK)

        for c in range(CHUNKS):
            cols = chunk_cols[c]
            pre = tile([P, PACK * CHUNK], BF16, "pre%d" % c)
            hid = tile([P, PACK * CHUNK], BF16, "hid%d" % c)
            h_codes = tile([P, CHUNK], U32, "h_codes%d" % c)
            h_sc = tile([P, CHUNK], U8, "h_sc%d" % c)
            if c < 2:
                pre_planes = pre[:].rearrange("p (t j) -> p t j", t=PACK)
                nc.vector.tensor_tensor(pre_planes, a_ps[c][:], tb_diff[:, :, cols], ALU.add)
                nc.scalar.activation(woven(hid[:], 4), by_plane(pre_planes, 4), ACT.Relu)
            else:
                nc.vector.tensor_tensor(
                    woven(pre[:], 2), by_plane(a_ps[c][:], 2), by_plane(tb_diff[:, :, cols], 2), ALU.add
                )
                nc.vector.tensor_scalar(hid[:], pre[:], 0.0, None, ALU.max)
            nc.vector.quantize_mx(out=h_codes[:].bitcast(E4), scales=h_sc[:], in_=hid[:])
            p_ps = psum.tile([P, N], F32, name="p_ps%d" % c)
            nc.tensor.matmul_mx(
                out=p_ps[:],
                lhsT=h_codes[:].bitcast(E4),
                lhsT_scale=h_sc[:],
                rhs=wb_codes[:].bitcast(E5),
                rhs_scale=wbs[:],
                start=True,
                stop=True,
            )
            neg_z = tile([P, N], F32, "neg_z%d" % c)
            low = tile([P, 1], F32, "low%d" % c)
            ea = tile([P, N], F32, "ea%d" % c)
            total = tile([P, 1], F32, "total%d" % c)
            inv = tile([P, 1], F32, "inv%d" % c)
            y = tile([P, N], F32, "y%d" % c)
            nc.vector.scalar_tensor_tensor(neg_z[:], p_ps[:], -0.7, bi_all[:], ALU.mult, ALU.subtract)
            nc.vector.tensor_reduce(low[:], neg_z[:], mybir.AxisListType.X, ALU.min)
            nc.scalar.activation(ea[:], neg_z[:], ACT.Exp, bias=low[:], scale=-1.0, accum_out=total[:])
            nc.vector.reciprocal(inv[:], total[:])
            nc.vector.tensor_scalar(y[:], ea[:], inv[:], 256.0, ALU.mult, ALU.mult)
            nc.sync.dma_start(out[cols, :], y[:])
